import numpy as np
import ml_dtypes


def mxq(x, axis, fmt="e4m3"):
    dtype, down = {"e4m3": (ml_dtypes.float8_e4m3fn, 7), "e5m2": (ml_dtypes.float8_e5m2, 14)}[fmt]
    v = np.moveaxis(np.asarray(x, np.float32).astype(ml_dtypes.bfloat16).astype(np.float64), axis, -1)
    blocks = v.reshape(v.shape[:-1] + (-1, 32))
    amax = np.abs(blocks).max(-1, keepdims=True)
    byte = np.maximum(np.where(amax > 0, np.frexp(amax)[1] - 1 + 127, 0) - down, 1)
    scale = np.exp2(byte - 127.0)
    codes = (blocks / scale).astype(np.float32).astype(dtype).astype(np.float64)
    return np.moveaxis((codes * scale).reshape(v.shape), -1, axis)


WIDE = False


def mx_kscale(k):
    if not WIDE:
        return np.ones(k)
    levels = np.array([10, -10, 5, -5, 0])
    if k % 512:
        return np.exp2(np.random.permutation(np.resize(levels, k // 32))).repeat(32)
    a = np.empty((k // 512, 16))
    for p in range(k // 512):
        a[p, :8] = np.random.permutation(np.resize(levels, 8))
        for g in range(8):
            far = levels[np.abs(levels - a[p, g]) >= 10]
            a[p, g + 8] = far[np.random.randint(len(far))]
    return np.exp2(a.ravel()).repeat(32)


def f64(x):
    return np.asarray(x).astype(np.float64)


def striped(idx):
    return np.tile(idx.reshape(-1, 16).T, (8, 1)).astype(np.uint16)


def unstriped(offs):
    return offs[:16].T.reshape(-1).astype(np.int64)


def striped8(idx):
    return np.concatenate([x.reshape(-1, 16).T for x in idx]).astype(np.uint16)


def runs(offs, k):
    lists = np.stack([offs[16 * r : 16 * r + 16].T.reshape(-1) for r in range(8)]).astype(np.int64)
    return lists[np.arange(k) % 512 // 64]


def pack_weight(w):
    k, n = w.shape
    w = f64(np.asarray(w, np.float32).astype(ml_dtypes.bfloat16)).reshape(k // 32, 32, n)
    amax = np.abs(w).max(1)
    byte = np.clip(np.where(amax > 0, np.frexp(amax)[1] - 1 + 127 - 7, 1), 1, 254)
    scaled = (w * np.exp2(127.0 - byte)[:, None, :]).reshape(k, n).astype(np.float32)
    words = np.ascontiguousarray(scaled.reshape(k // 512, 128, 4, n).transpose(0, 1, 3, 2)).astype(ml_dtypes.float8_e4m3fn).view(np.uint8)
    return words, np.ascontiguousarray(byte.astype(np.uint8).reshape(k // 512, 16, n))


def unpack_weight(words, scales):
    g, p, n, _ = words.shape
    vals = np.ascontiguousarray(words).view(ml_dtypes.float8_e4m3fn).astype(np.float64) * np.repeat(np.exp2(scales.astype(np.float64) - 127.0), 8, axis=1)[..., None]
    return vals.transpose(0, 1, 3, 2).reshape(g * 512, n)


K, T, S, V, U, H = 512, 2048, 512, 512, 1024, 512


def setup_inputs():
    n = np.random.standard_normal
    s = mx_kscale(K)[:, None]
    u = mx_kscale(S)
    packed_xT = pack_weight(n((K, T)) * s)
    return {
        "x_words": packed_xT[0],
        "x_scales": packed_xT[1],
        "w1": (n((K, H)) / np.sqrt(K) / s).astype(np.float32),
        "w2": (n((K, H)) / np.sqrt(K) / s).astype(np.float32),
        "ga": (np.random.uniform(0.5, 1.5, (H, 1)) * u[:, None]).astype(np.float32),
        "gb": (np.random.uniform(0.5, 1.5, (H, 1)) / u[:, None]).astype(np.float32),
        "page": n((S, U)).astype(np.float32),
        "offs": striped(np.random.permutation(T)[:S]),
        "two": striped(np.random.permutation(T)[:V]),
        "slot": striped8(np.stack([np.random.permutation(U)[:V] for _ in range(8)])),
    }


def reference(x_words, x_scales, w1, w2, ga, gb, page, offs, two, slot):
    xq = unpack_weight(x_words, x_scales)[:, unstriped(offs)]
    a = mxq(f64(w1), 0, "e4m3").T @ xq
    z = f64(ga) * a
    x_two = unpack_weight(x_words, x_scales)[:, unstriped(two)]
    b = mxq(f64(w2), 0, "e4m3").T @ x_two
    z2 = f64(gb) * b
    cv = 0.0625 * ((mxq(z, 0, "e4m3").T @ mxq(z2, 0, "e4m3")))
    tc = np.tanh(cv)
    out = f64(page).copy()
    out[np.arange(S)[:, None], runs(slot, S)] = tc
    return out

@@ -1,0 +1,185 @@
+from contextlib import ExitStack
+
+import concourse.mybir as mybir
+
+K, T, S, V, U, H = 512, 2048, 512, 512, 1024, 512
+FLOPS = 2 * K * H * S + 2 * K * H * V + 2 * H * S * V
+
+F32 = mybir.dt.float32
+BF16 = mybir.dt.bfloat16
+I32 = mybir.dt.int32
+U32 = mybir.dt.uint32
+U16 = mybir.dt.uint16
+U8 = mybir.dt.uint8
+FP8X4 = mybir.dt.float8_e4m3fn_x4
+ACT = mybir.ActivationFunctionType
+ALU = mybir.AluOpType
+
+P = 128
+PACK = 4
+HALF = V // 2
+W2_SCALAR = 48
+
+
+def tile_picked_momput_none_p_kernel(
+    tc, x_words, x_scales, w1, w2, ga, gb, page, offs, two, slot, out
+):
+    nc = tc.nc
+    with ExitStack() as ctx:
+        keep = ctx.enter_context(tc.tile_pool(name="keep", bufs=1))
+        psum = ctx.enter_context(tc.psum_pool(name="psum", bufs=1))
+
+        def sb(name, shape, dtype, tag=None):
+            return keep.tile(shape, dtype, name=name, tag=tag or name, align_bytes=64)
+
+        def bank(i, shape):
+            return psum.tile(shape, F32, name="bank%d" % i)
+
+        def product(dst, lhs_codes, lhs_scales, rhs_codes, rhs_scales):
+            nc.tensor.matmul_mx(
+                out=dst,
+                lhsT=lhs_codes.bitcast(FP8X4),
+                lhsT_scale=lhs_scales,
+                rhs=rhs_codes.bitcast(FP8X4),
+                rhs_scale=rhs_scales,
+                start=True,
+                stop=True,
+            )
+
+        two_list = sb("two_list", [P, V // 16], U16)
+        offs_list = sb("offs_list", [P, S // 16], U16)
+        slot_list = sb("slot_list", [P, V // 16], U16)
+        x_table = sb("x_table", [P, T], U32)
+        x_scale_table = sb("x_scale_table", [P, T], U8)
+        w1_raw = sb("w1_raw", [P, PACK, H], F32)
+        w2_raw = sb("w2_raw", [P, PACK, H], F32)
+        ga_t = sb("ga_t", [P, PACK], F32)
+        gb_t = sb("gb_t", [P, PACK], F32)
+        windows = [sb("window%d" % t, [P, U], F32) for t in range(PACK)]
+
+        nc.vector.memset(x_scale_table[:].bitcast(I32), 0)
+        nc.sync.dma_start(two_list[:], two)
+        nc.sync.dma_start(offs_list[:], offs)
+        for q in range(4):
+            nc.sync.dma_start(
+                x_scale_table[32 * q : 32 * q + 4, :].bitcast(I32),
+                x_scales[0, 4 * q : 4 * q + 4, :].bitcast(I32),
+            )
+        nc.sync.dma_start(w2_raw[:], w2.rearrange("(p k) h -> p k h", k=PACK))
+        nc.sync.dma_start(x_table[:].bitcast(I32), x_words[0].rearrange("p n r -> p (n r)").bitcast(I32))
+        nc.sync.dma_start(w1_raw[:], w1.rearrange("(p k) h -> p k h", k=PACK))
+        nc.sync.dma_start(gb_t[:], gb.rearrange("(p j) o -> p (j o)", j=PACK))
+        nc.sync.dma_start(ga_t[:], ga.rearrange("(p j) o -> p (j o)", j=PACK))
+        nc.sync.dma_start(slot_list[:], slot)
+        page_rows = page.rearrange("(p t) u -> t p u", t=PACK)
+        out_rows = out.rearrange("(p t) u -> t p u", t=PACK)
+        for t in range(PACK):
+            nc.sync.dma_start(windows[t][:], page_rows[t])
+
+        two_scales = sb("two_scales", [P, V], U8)
+        offs_scales = sb("offs_scales", [P, S], U8)
+        nc.vector.tensor_copy(two_scales[:], x_scale_table[:].indirect(two_list[:]))
+        nc.vector.tensor_copy(
+            offs_scales[:].rearrange("p (t m) -> p m t", t=PACK), x_scale_table[:].indirect(offs_list[:])
+        )
+
+        def weights(name, raw, scalar_share):
+            grouped = sb(name + "_grouped", [P, PACK * H], BF16)
+            dst = grouped[:].rearrange("p (j m k) -> p m k j", j=PACK, k=PACK)
+            src = raw[:].rearrange("p k (m j) -> p m k j", j=PACK)
+            if scalar_share:
+                nc.scalar.copy(dst[:, :scalar_share], src[:, :scalar_share])
+            nc.vector.tensor_copy(dst[:, scalar_share:], src[:, scalar_share:])
+            codes = sb(name + "_codes", [P, H], U32)
+            scales = sb(name + "_scales", [P, H], U8)
+            nc.vector.quantize_mx(out=codes[:].bitcast(FP8X4), scales=scales[:], in_=grouped[:])
+            return codes, scales
+
+        w2_codes, w2_scales = weights("w2", w2_raw, W2_SCALAR)
+        picked_words = sb("picked_words", [P, V + S], U32, tag="w2_grouped")
+        two_words = picked_words[:, :V]
+        offs_words = picked_words[:, V:]
+        nc.vector.tensor_copy(two_words, x_table[:].indirect(two_list[:]))
+        nc.vector.tensor_copy(
+            offs_words.rearrange("p (t m) -> p m t", t=PACK), x_table[:].indirect(offs_list[:])
+        )
+
+        z2_planes = []
+        for h in range(2):
+            cols = slice(h * HALF, (h + 1) * HALF)
+            planes = sb("z2_planes%d" % h, [P, PACK, HALF], BF16)
+            for u in range(2):
+                acc = bank(2 * h + u, [P, 2, HALF])
+                for e in range(2):
+                    j = 2 * u + e
+                    feats = slice(j * P, (j + 1) * P)
+                    product(acc[:, e, :], w2_codes[:, feats], w2_scales[:, feats], two_words[:, cols], two_scales[:, cols])
+                for e in range(2):
+                    j = 2 * u + e
+                    nc.scalar.activation(out=planes[:, j, :], in_=acc[:, e, :], func=ACT.Copy, scale=gb_t[:, j : j + 1])
+            z2_planes.append(planes)
+
+        w1_codes, w1_scales = weights("w1", w1_raw, 0)
+
+        a_banks = []
+        for t in range(PACK):
+            cols = slice(t * P, (t + 1) * P)
+            acc = bank(4 + t, [P, PACK, P])
+            for j in range(PACK):
+                feats = slice(j * P, (j + 1) * P)
+                product(acc[:, j, :], w1_codes[:, feats], w1_scales[:, feats], offs_words[:, cols], offs_scales[:, cols])
+            a_banks.append(acc)
+
+        def interleave(copy, grouped, planes):
+            copy(
+                grouped[:].rearrange("p (c i j) -> p c j i", i=4, j=PACK),
+                planes[:].rearrange("p j (c i) -> p c j i", i=4),
+            )
+
+        z2_codes = sb("z2_codes", [P, V], U32)
+        z2_scales = sb("z2_scales", [P, V], U8)
+        z2_grouped = [sb("z2_grouped%d" % h, [P, PACK * HALF], BF16) for h in range(2)]
+
+        def quantize_z2(h):
+            cols = slice(h * HALF, (h + 1) * HALF)
+            nc.vector.quantize_mx(out=z2_codes[:, cols].bitcast(FP8X4), scales=z2_scales[:, cols], in_=z2_grouped[h][:])
+
+        z_grouped = [sb("z_grouped%d" % t, [P, PACK * P], BF16) for t in range(PACK)]
+        z_codes = [sb("z_codes%d" % t, [P, P], U32) for t in range(PACK)]
+        z_scales = [sb("z_scales%d" % t, [P, P], U8) for t in range(PACK)]
+
+        def weigh_on_scalar(t):
+            planes = sb("z_planes%d" % t, [P, PACK, P], BF16)
+            for j in range(PACK):
+                nc.scalar.activation(out=planes[:, j, :], in_=a_banks[t][:, j, :], func=ACT.Copy, scale=ga_t[:, j : j + 1])
+            interleave(nc.scalar.copy, z_grouped[t], planes)
+
+        def quantize_z(t):
+            nc.vector.quantize_mx(out=z_codes[t][:].bitcast(FP8X4), scales=z_scales[t][:], in_=z_grouped[t][:])
+
+        interleave(nc.vector.tensor_copy, z2_grouped[0], z2_planes[0])
+        nc.vector.tensor_tensor(
+            out=z_grouped[0][:].rearrange("p (m j) -> p m j", j=PACK),
+            in0=a_banks[0][:].rearrange("p j m -> p m j"),
+            in1=ga_t[:].unsqueeze(1).to_broadcast([P, P, PACK]),
+            op=ALU.mult,
+        )
+        quantize_z2(0)
+        quantize_z(0)
+        interleave(nc.vector.tensor_copy, z2_grouped[1], z2_planes[1])
+        quantize_z2(1)
+
+        for t in range(PACK):
+            scores = [bank(2 * (t % 2) + h, [P, HALF]) for h in range(2)]
+            for h in range(2):
+                cols = slice(h * HALF, (h + 1) * HALF)
+                product(scores[h][:], z_codes[t][:], z_scales[t][:], z2_codes[:, cols], z2_scales[:, cols])
+            for h in range(2):
+                tanh = sb("tanh%d_%d" % (t, h), [P, HALF], F32, tag="z_planes%d" % (t + 1) if h else None)
+                nc.scalar.activation(out=tanh[:], in_=scores[h][:], func=ACT.Tanh, scale=0.0625)
+                places = windows[t][:].indirect(slot_list[:, h * HALF // 16 : (h + 1) * HALF // 16])
+                nc.vector.tensor_copy(places, tanh[:])
+                if h == 0 and t + 1 < PACK:
+                    weigh_on_scalar(t + 1)
+                    quantize_z(t + 1)
+            nc.sync.dma_start(out_rows[t], windows[t][:])

@@ -18,7 +18,7 @@ ALU = mybir.AluOpType
 P = 128
 PACK = 4
 HALF = V // 2
-W2_SCALAR = 48
+W2_SCALAR = 88
 
 
 def tile_picked_momput_none_p_kernel(
@@ -51,25 +51,27 @@ def tile_picked_momput_none_p_kernel(
         slot_list = sb("slot_list", [P, V // 16], U16)
         x_table = sb("x_table", [P, T], U32)
         x_scale_table = sb("x_scale_table", [P, T], U8)
-        w1_raw = sb("w1_raw", [P, PACK, H], F32)
+        w1_raw = [sb("w1_raw%d" % h, [P, PACK, H // 2], F32) for h in range(2)]
         w2_raw = sb("w2_raw", [P, PACK, H], F32)
         ga_t = sb("ga_t", [P, PACK], F32)
         gb_t = sb("gb_t", [P, PACK], F32)
         windows = [sb("window%d" % t, [P, U], F32) for t in range(PACK)]
 
         nc.vector.memset(x_scale_table[:].bitcast(I32), 0)
+        nc.sync.dma_start(w2_raw[:], w2.rearrange("(p k) h -> p k h", k=PACK))
         nc.sync.dma_start(two_list[:], two)
         nc.sync.dma_start(offs_list[:], offs)
         for q in range(4):
-            nc.sync.dma_start(
+            nc.scalar.dma_start(
                 x_scale_table[32 * q : 32 * q + 4, :].bitcast(I32),
                 x_scales[0, 4 * q : 4 * q + 4, :].bitcast(I32),
             )
-        nc.sync.dma_start(w2_raw[:], w2.rearrange("(p k) h -> p k h", k=PACK))
         nc.sync.dma_start(x_table[:].bitcast(I32), x_words[0].rearrange("p n r -> p (n r)").bitcast(I32))
-        nc.sync.dma_start(w1_raw[:], w1.rearrange("(p k) h -> p k h", k=PACK))
-        nc.sync.dma_start(gb_t[:], gb.rearrange("(p j) o -> p (j o)", j=PACK))
-        nc.sync.dma_start(ga_t[:], ga.rearrange("(p j) o -> p (j o)", j=PACK))
+        w1_rows = w1.rearrange("(p k) h -> p k h", k=PACK)
+        for h in range(2):
+            nc.sync.dma_start(w1_raw[h][:], w1_rows[:, :, h * H // 2 : (h + 1) * H // 2])
+        nc.gpsimd.dma_start(gb_t[:], gb.rearrange("(p j) o -> p (j o)", j=PACK))
+        nc.gpsimd.dma_start(ga_t[:], ga.rearrange("(p j) o -> p (j o)", j=PACK))
         nc.sync.dma_start(slot_list[:], slot)
         page_rows = page.rearrange("(p t) u -> t p u", t=PACK)
         out_rows = out.rearrange("(p t) u -> t p u", t=PACK)
@@ -83,19 +85,28 @@ def tile_picked_momput_none_p_kernel(
             offs_scales[:].rearrange("p (t m) -> p m t", t=PACK), x_scale_table[:].indirect(offs_list[:])
         )
 
-        def weights(name, raw, scalar_share):
+        def weights(name, scalar_raw, vector_raw, pieces):
             grouped = sb(name + "_grouped", [P, PACK * H], BF16)
             dst = grouped[:].rearrange("p (j m k) -> p m k j", j=PACK, k=PACK)
-            src = raw[:].rearrange("p k (m j) -> p m k j", j=PACK)
-            if scalar_share:
-                nc.scalar.copy(dst[:, :scalar_share], src[:, :scalar_share])
-            nc.vector.tensor_copy(dst[:, scalar_share:], src[:, scalar_share:])
+            cut = scalar_raw.shape[2] // PACK
+            nc.scalar.copy(dst[:, :cut], scalar_raw.rearrange("p k (m j) -> p m k j", j=PACK))
+            step = PACK // pieces
+            if vector_raw is not None:
+                src = vector_raw.rearrange("p k (m j) -> p m k j", j=PACK)
+                for j in range(0, PACK, step):
+                    nc.vector.tensor_copy(dst[:, cut:, :, j : j + step], src[:, :, :, j : j + step])
             codes = sb(name + "_codes", [P, H], U32)
             scales = sb(name + "_scales", [P, H], U8)
-            nc.vector.quantize_mx(out=codes[:].bitcast(FP8X4), scales=scales[:], in_=grouped[:])
+            for j in range(0, PACK, step):
+                cols = slice(j * P, (j + step) * P)
+                nc.vector.quantize_mx(
+                    out=codes[:, cols].bitcast(FP8X4),
+                    scales=scales[:, cols],
+                    in_=grouped[:, PACK * cols.start : PACK * cols.stop],
+                )
             return codes, scales
 
-        w2_codes, w2_scales = weights("w2", w2_raw, W2_SCALAR)
+        w2_codes, w2_scales = weights("w2", w2_raw[:, :, : PACK * W2_SCALAR], w2_raw[:, :, PACK * W2_SCALAR :], 1)
         picked_words = sb("picked_words", [P, V + S], U32, tag="w2_grouped")
         two_words = picked_words[:, :V]
         offs_words = picked_words[:, V:]
@@ -104,10 +115,11 @@ def tile_picked_momput_none_p_kernel(
             offs_words.rearrange("p (t m) -> p m t", t=PACK), x_table[:].indirect(offs_list[:])
         )
 
-        z2_planes = []
+        w1_codes, w1_scales = weights("w1", w1_raw[0][:], w1_raw[1][:], 2)
+
+        z2_planes = sb("z2_planes", [P, 2, PACK, HALF], BF16, tag="w1_raw0")
         for h in range(2):
             cols = slice(h * HALF, (h + 1) * HALF)
-            planes = sb("z2_planes%d" % h, [P, PACK, HALF], BF16)
             for u in range(2):
                 acc = bank(2 * h + u, [P, 2, HALF])
                 for e in range(2):
@@ -116,24 +128,20 @@ def tile_picked_momput_none_p_kernel(
                     product(acc[:, e, :], w2_codes[:, feats], w2_scales[:, feats], two_words[:, cols], two_scales[:, cols])
                 for e in range(2):
                     j = 2 * u + e
-                    nc.scalar.activation(out=planes[:, j, :], in_=acc[:, e, :], func=ACT.Copy, scale=gb_t[:, j : j + 1])
-            z2_planes.append(planes)
+                    nc.scalar.activation(out=z2_planes[:, h, j, :], in_=acc[:, e, :], func=ACT.Copy, scale=gb_t[:, j : j + 1])
 
-        w1_codes, w1_scales = weights("w1", w1_raw, 0)
-
-        a_banks = []
-        for t in range(PACK):
+        def project_a(t):
             cols = slice(t * P, (t + 1) * P)
-            acc = bank(4 + t, [P, PACK, P])
+            acc = bank(4 + min(t, 1), [P, PACK, P])
             for j in range(PACK):
                 feats = slice(j * P, (j + 1) * P)
                 product(acc[:, j, :], w1_codes[:, feats], w1_scales[:, feats], offs_words[:, cols], offs_scales[:, cols])
-            a_banks.append(acc)
+            return acc
 
         def interleave(copy, grouped, planes):
             copy(
                 grouped[:].rearrange("p (c i j) -> p c j i", i=4, j=PACK),
-                planes[:].rearrange("p j (c i) -> p c j i", i=4),
+                planes.rearrange("p j (c i) -> p c j i", i=4),
             )
 
         z2_codes = sb("z2_codes", [P, V], U32)
@@ -149,37 +157,42 @@ def tile_picked_momput_none_p_kernel(
         z_scales = [sb("z_scales%d" % t, [P, P], U8) for t in range(PACK)]
 
         def weigh_on_scalar(t):
-            planes = sb("z_planes%d" % t, [P, PACK, P], BF16)
+            acc = project_a(t)
+            planes = sb("z_planes%d" % t, [P, PACK, P], BF16, tag="z_grouped0" if t == 1 else None)
             for j in range(PACK):
-                nc.scalar.activation(out=planes[:, j, :], in_=a_banks[t][:, j, :], func=ACT.Copy, scale=ga_t[:, j : j + 1])
-            interleave(nc.scalar.copy, z_grouped[t], planes)
+                nc.scalar.activation(out=planes[:, j, :], in_=acc[:, j, :], func=ACT.Copy, scale=ga_t[:, j : j + 1])
+            interleave(nc.scalar.copy, z_grouped[t], planes[:])
 
         def quantize_z(t):
             nc.vector.quantize_mx(out=z_codes[t][:].bitcast(FP8X4), scales=z_scales[t][:], in_=z_grouped[t][:])
 
-        interleave(nc.vector.tensor_copy, z2_grouped[0], z2_planes[0])
+        interleave(nc.vector.tensor_copy, z2_grouped[0], z2_planes[:, 0])
+        interleave(nc.scalar.copy, z2_grouped[1], z2_planes[:, 1])
         nc.vector.tensor_tensor(
             out=z_grouped[0][:].rearrange("p (m j) -> p m j", j=PACK),
-            in0=a_banks[0][:].rearrange("p j m -> p m j"),
+            in0=project_a(0)[:].rearrange("p j m -> p m j"),
             in1=ga_t[:].unsqueeze(1).to_broadcast([P, P, PACK]),
             op=ALU.mult,
         )
         quantize_z2(0)
         quantize_z(0)
-        interleave(nc.vector.tensor_copy, z2_grouped[1], z2_planes[1])
         quantize_z2(1)
 
+        def put(t, cols, bank_index, tag):
+            width = cols.stop - cols.start
+            scores = bank(bank_index, [P, width])
+            product(scores[:], z_codes[t][:], z_scales[t][:], z2_codes[:, cols], z2_scales[:, cols])
+            tanh = sb("tanh%d_%d" % (t, cols.start), [P, width], F32, tag=tag)
+            nc.scalar.activation(out=tanh[:], in_=scores[:], func=ACT.Tanh, scale=0.0625)
+            nc.vector.tensor_copy(windows[t][:].indirect(slot_list[:, cols.start // 16 : cols.stop // 16]), tanh[:])
+
         for t in range(PACK):
-            scores = [bank(2 * (t % 2) + h, [P, HALF]) for h in range(2)]
-            for h in range(2):
-                cols = slice(h * HALF, (h + 1) * HALF)
-                product(scores[h][:], z_codes[t][:], z_scales[t][:], z2_codes[:, cols], z2_scales[:, cols])
-            for h in range(2):
-                tanh = sb("tanh%d_%d" % (t, h), [P, HALF], F32, tag="z_planes%d" % (t + 1) if h else None)
-                nc.scalar.activation(out=tanh[:], in_=scores[h][:], func=ACT.Tanh, scale=0.0625)
-                places = windows[t][:].indirect(slot_list[:, h * HALF // 16 : (h + 1) * HALF // 16])
-                nc.vector.tensor_copy(places, tanh[:])
-                if h == 0 and t + 1 < PACK:
-                    weigh_on_scalar(t + 1)
-                    quantize_z(t + 1)
+            halved = t < 2
+            if halved:
+                put(t, slice(0, HALF), 6 - 6 * t, None)
+            if t + 1 < PACK:
+                weigh_on_scalar(t + 1)
+                quantize_z(t + 1)
+            tag = "z_grouped0" if t == 0 else "z_planes%d" % (t + 1)
+            put(t, slice(HALF if halved else 0, V), [7, 1, 2, 3][t], tag)
             nc.sync.dma_start(out_rows[t], windows[t][:])

@@ -18,7 +18,6 @@ ALU = mybir.AluOpType
 P = 128
 PACK = 4
 HALF = V // 2
-W2_SCALAR = 88
 
 
 def tile_picked_momput_none_p_kernel(
@@ -52,26 +51,28 @@ def tile_picked_momput_none_p_kernel(
         x_table = sb("x_table", [P, T], U32)
         x_scale_table = sb("x_scale_table", [P, T], U8)
         w1_raw = [sb("w1_raw%d" % h, [P, PACK, H // 2], F32) for h in range(2)]
-        w2_raw = sb("w2_raw", [P, PACK, H], F32)
+        w2_raw = [sb("w2_raw%d" % h, [P, PACK, H // 2], F32) for h in range(2)]
         ga_t = sb("ga_t", [P, PACK], F32)
         gb_t = sb("gb_t", [P, PACK], F32)
         windows = [sb("window%d" % t, [P, U], F32) for t in range(PACK)]
 
         nc.vector.memset(x_scale_table[:].bitcast(I32), 0)
-        nc.sync.dma_start(w2_raw[:], w2.rearrange("(p k) h -> p k h", k=PACK))
+        w2_rows = w2.rearrange("(p k) h -> p k h", k=PACK)
         nc.sync.dma_start(two_list[:], two)
+        nc.sync.dma_start(w2_raw[0][:], w2_rows[:, :, : H // 2])
         nc.sync.dma_start(offs_list[:], offs)
         for q in range(4):
-            nc.scalar.dma_start(
+            nc.sync.dma_start(
                 x_scale_table[32 * q : 32 * q + 4, :].bitcast(I32),
                 x_scales[0, 4 * q : 4 * q + 4, :].bitcast(I32),
             )
+        nc.sync.dma_start(w2_raw[1][:], w2_rows[:, :, H // 2 :])
         nc.sync.dma_start(x_table[:].bitcast(I32), x_words[0].rearrange("p n r -> p (n r)").bitcast(I32))
+        nc.sync.dma_start(gb_t[:], gb.rearrange("(p j) o -> p (j o)", j=PACK))
         w1_rows = w1.rearrange("(p k) h -> p k h", k=PACK)
         for h in range(2):
             nc.sync.dma_start(w1_raw[h][:], w1_rows[:, :, h * H // 2 : (h + 1) * H // 2])
-        nc.gpsimd.dma_start(gb_t[:], gb.rearrange("(p j) o -> p (j o)", j=PACK))
-        nc.gpsimd.dma_start(ga_t[:], ga.rearrange("(p j) o -> p (j o)", j=PACK))
+        nc.sync.dma_start(ga_t[:], ga.rearrange("(p j) o -> p (j o)", j=PACK))
         nc.sync.dma_start(slot_list[:], slot)
         page_rows = page.rearrange("(p t) u -> t p u", t=PACK)
         out_rows = out.rearrange("(p t) u -> t p u", t=PACK)
@@ -79,26 +80,22 @@ def tile_picked_momput_none_p_kernel(
             nc.sync.dma_start(windows[t][:], page_rows[t])
 
         two_scales = sb("two_scales", [P, V], U8)
-        offs_scales = sb("offs_scales", [P, S], U8)
         nc.vector.tensor_copy(two_scales[:], x_scale_table[:].indirect(two_list[:]))
+
+        offs_scales = sb("offs_scales", [P, S], U8)
         nc.vector.tensor_copy(
             offs_scales[:].rearrange("p (t m) -> p m t", t=PACK), x_scale_table[:].indirect(offs_list[:])
         )
 
-        def weights(name, scalar_raw, vector_raw, pieces):
-            grouped = sb(name + "_grouped", [P, PACK * H], BF16)
+        def deal(copy, grouped, first, raw, tiles=slice(0, PACK)):
+            count = raw.shape[2] // PACK
             dst = grouped[:].rearrange("p (j m k) -> p m k j", j=PACK, k=PACK)
-            cut = scalar_raw.shape[2] // PACK
-            nc.scalar.copy(dst[:, :cut], scalar_raw.rearrange("p k (m j) -> p m k j", j=PACK))
-            step = PACK // pieces
-            if vector_raw is not None:
-                src = vector_raw.rearrange("p k (m j) -> p m k j", j=PACK)
-                for j in range(0, PACK, step):
-                    nc.vector.tensor_copy(dst[:, cut:, :, j : j + step], src[:, :, :, j : j + step])
+            copy(dst[:, first : first + count, :, tiles], raw.rearrange("p k (m j) -> p m k j", j=PACK)[:, :, :, tiles])
+
+        def quantize_weights(name, grouped, pieces):
             codes = sb(name + "_codes", [P, H], U32)
             scales = sb(name + "_scales", [P, H], U8)
-            for j in range(0, PACK, step):
-                cols = slice(j * P, (j + step) * P)
+            for cols in pieces:
                 nc.vector.quantize_mx(
                     out=codes[:, cols].bitcast(FP8X4),
                     scales=scales[:, cols],
@@ -106,16 +103,22 @@ def tile_picked_momput_none_p_kernel(
                 )
             return codes, scales
 
-        w2_codes, w2_scales = weights("w2", w2_raw[:, :, : PACK * W2_SCALAR], w2_raw[:, :, PACK * W2_SCALAR :], 1)
+        w2_grouped = sb("w2_grouped", [P, PACK * H], BF16)
+        for h in range(2):
+            deal(nc.scalar.copy, w2_grouped, h * P // 2, w2_raw[h][:])
+        w2_codes, w2_scales = quantize_weights("w2", w2_grouped, [slice(0, H)])
+
         picked_words = sb("picked_words", [P, V + S], U32, tag="w2_grouped")
         two_words = picked_words[:, :V]
         offs_words = picked_words[:, V:]
         nc.vector.tensor_copy(two_words, x_table[:].indirect(two_list[:]))
-        nc.vector.tensor_copy(
-            offs_words.rearrange("p (t m) -> p m t", t=PACK), x_table[:].indirect(offs_list[:])
-        )
+        nc.vector.tensor_copy(offs_words.rearrange("p (t m) -> p m t", t=PACK), x_table[:].indirect(offs_list[:]))
 
-        w1_codes, w1_scales = weights("w1", w1_raw[0][:], w1_raw[1][:], 2)
+        w1_grouped = sb("w1_grouped", [P, PACK * H], BF16)
+        deal(nc.scalar.copy, w1_grouped, 0, w1_raw[0][:])
+        for j in (0, 2):
+            deal(nc.vector.tensor_copy, w1_grouped, P // 2, w1_raw[1][:], slice(j, j + 2))
+        w1_codes, w1_scales = quantize_weights("w1", w1_grouped, [slice(0, H // 2), slice(H // 2, H)])
 
         z2_planes = sb("z2_planes", [P, 2, PACK, HALF], BF16, tag="w1_raw0")
         for h in range(2):

@@ -61,11 +61,8 @@ def tile_picked_momput_none_p_kernel(
         nc.sync.dma_start(two_list[:], two)
         nc.sync.dma_start(w2_raw[0][:], w2_rows[:, :, : H // 2])
         nc.sync.dma_start(offs_list[:], offs)
-        for q in range(4):
-            nc.sync.dma_start(
-                x_scale_table[32 * q : 32 * q + 4, :].bitcast(I32),
-                x_scales[0, 4 * q : 4 * q + 4, :].bitcast(I32),
-            )
+        for r in range(4):
+            nc.sync.dma_start(x_scale_table[r:P:32, :].bitcast(I32), x_scales[0, r:16:4, :].bitcast(I32))
         nc.sync.dma_start(w2_raw[1][:], w2_rows[:, :, H // 2 :])
         nc.sync.dma_start(x_table[:].bitcast(I32), x_words[0].rearrange("p n r -> p (n r)").bitcast(I32))
         nc.sync.dma_start(gb_t[:], gb.rearrange("(p j) o -> p (j o)", j=PACK))

@@ -84,10 +84,12 @@ def tile_picked_momput_none_p_kernel(
             offs_scales[:].rearrange("p (t m) -> p m t", t=PACK), x_scale_table[:].indirect(offs_list[:])
         )
 
-        def deal(copy, grouped, first, raw, tiles=slice(0, PACK)):
+        def deal(copy, grouped, first, raw):
             count = raw.shape[2] // PACK
             dst = grouped[:].rearrange("p (j m k) -> p m k j", j=PACK, k=PACK)
-            copy(dst[:, first : first + count, :, tiles], raw.rearrange("p k (m j) -> p m k j", j=PACK)[:, :, :, tiles])
+            src = raw.rearrange("p k (m j) -> p m k j", j=PACK)
+            for j in (0, 2):
+                copy(dst[:, first : first + count, :, j : j + 2], src[:, :, :, j : j + 2])
 
         def quantize_weights(name, grouped, pieces):
             codes = sb(name + "_codes", [P, H], U32)
@@ -113,8 +115,7 @@ def tile_picked_momput_none_p_kernel(
 
         w1_grouped = sb("w1_grouped", [P, PACK * H], BF16)
         deal(nc.scalar.copy, w1_grouped, 0, w1_raw[0][:])
-        for j in (0, 2):
-            deal(nc.vector.tensor_copy, w1_grouped, P // 2, w1_raw[1][:], slice(j, j + 2))
+        deal(nc.vector.tensor_copy, w1_grouped, P // 2, w1_raw[1][:])
         w1_codes, w1_scales = quantize_weights("w1", w1_grouped, [slice(0, H // 2), slice(H // 2, H)])
 
         z2_planes = sb("z2_planes", [P, 2, PACK, HALF], BF16, tag="w1_raw0")

from contextlib import ExitStack

import concourse.mybir as mybir

K, T, S, V, U, H = 512, 2048, 512, 512, 1024, 512
FLOPS = 2 * K * H * S + 2 * K * H * V + 2 * H * S * V

F32 = mybir.dt.float32
BF16 = mybir.dt.bfloat16
I32 = mybir.dt.int32
U32 = mybir.dt.uint32
U16 = mybir.dt.uint16
U8 = mybir.dt.uint8
FP8X4 = mybir.dt.float8_e4m3fn_x4
ACT = mybir.ActivationFunctionType
ALU = mybir.AluOpType

P = 128
PACK = 4
HALF = V // 2


def tile_picked_momput_none_p_kernel(
    tc, x_words, x_scales, w1, w2, ga, gb, page, offs, two, slot, out
):
    nc = tc.nc
    with ExitStack() as ctx:
        keep = ctx.enter_context(tc.tile_pool(name="keep", bufs=1))
        psum = ctx.enter_context(tc.psum_pool(name="psum", bufs=1))

        def sb(name, shape, dtype, tag=None):
            return keep.tile(shape, dtype, name=name, tag=tag or name, align_bytes=64)

        def bank(i, shape):
            return psum.tile(shape, F32, name="bank%d" % i)

        def product(dst, lhs_codes, lhs_scales, rhs_codes, rhs_scales):
            nc.tensor.matmul_mx(
                out=dst,
                lhsT=lhs_codes.bitcast(FP8X4),
                lhsT_scale=lhs_scales,
                rhs=rhs_codes.bitcast(FP8X4),
                rhs_scale=rhs_scales,
                start=True,
                stop=True,
            )

        two_list = sb("two_list", [P, V // 16], U16)
        offs_list = sb("offs_list", [P, S // 16], U16)
        slot_list = sb("slot_list", [P, V // 16], U16)
        x_table = sb("x_table", [P, T], U32)
        x_scale_table = sb("x_scale_table", [P, T], U8)
        w1_raw = [sb("w1_raw%d" % h, [P, PACK, H // 2], F32) for h in range(2)]
        w2_raw = [sb("w2_raw%d" % h, [P, PACK, H // 2], F32) for h in range(2)]
        ga_t = sb("ga_t", [P, PACK], F32)
        gb_t = sb("gb_t", [P, PACK], F32)
        windows = [sb("window%d" % t, [P, U], F32) for t in range(PACK)]

        nc.vector.memset(x_scale_table[:].bitcast(I32), 0)
        w2_rows = w2.rearrange("(p k) h -> p k h", k=PACK)
        nc.sync.dma_start(two_list[:], two)
        nc.sync.dma_start(w2_raw[0][:], w2_rows[:, :, : H // 2])
        nc.sync.dma_start(offs_list[:], offs)
        for r in range(4):
            nc.sync.dma_start(x_scale_table[r:P:32, :].bitcast(I32), x_scales[0, r:16:4, :].bitcast(I32))
        nc.sync.dma_start(w2_raw[1][:], w2_rows[:, :, H // 2 :])
        nc.sync.dma_start(x_table[:].bitcast(I32), x_words[0].rearrange("p n r -> p (n r)").bitcast(I32))
        nc.sync.dma_start(gb_t[:], gb.rearrange("(p j) o -> p (j o)", j=PACK))
        w1_rows = w1.rearrange("(p k) h -> p k h", k=PACK)
        for h in range(2):
            nc.sync.dma_start(w1_raw[h][:], w1_rows[:, :, h * H // 2 : (h + 1) * H // 2])
        nc.sync.dma_start(ga_t[:], ga.rearrange("(p j) o -> p (j o)", j=PACK))
        nc.sync.dma_start(slot_list[:], slot)
        page_rows = page.rearrange("(p t) u -> t p u", t=PACK)
        out_rows = out.rearrange("(p t) u -> t p u", t=PACK)
        for t in range(PACK):
            nc.sync.dma_start(windows[t][:], page_rows[t])

        two_scales = sb("two_scales", [P, V], U8)
        nc.vector.tensor_copy(two_scales[:], x_scale_table[:].indirect(two_list[:]))

        offs_scales = sb("offs_scales", [P, S], U8)
        nc.vector.tensor_copy(
            offs_scales[:].rearrange("p (t m) -> p m t", t=PACK), x_scale_table[:].indirect(offs_list[:])
        )

        def deal(copy, grouped, first, raw):
            count = raw.shape[2] // PACK
            dst = grouped[:].rearrange("p (j m k) -> p m k j", j=PACK, k=PACK)
            src = raw.rearrange("p k (m j) -> p m k j", j=PACK)
            for j in (0, 2):
                copy(dst[:, first : first + count, :, j : j + 2], src[:, :, :, j : j + 2])

        def quantize_weights(name, grouped, pieces):
            codes = sb(name + "_codes", [P, H], U32)
            scales = sb(name + "_scales", [P, H], U8)
            for cols in pieces:
                nc.vector.quantize_mx(
                    out=codes[:, cols].bitcast(FP8X4),
                    scales=scales[:, cols],
                    in_=grouped[:, PACK * cols.start : PACK * cols.stop],
                )
            return codes, scales

        w2_grouped = sb("w2_grouped", [P, PACK * H], BF16)
        for h in range(2):
            deal(nc.scalar.copy, w2_grouped, h * P // 2, w2_raw[h][:])
        w2_codes, w2_scales = quantize_weights("w2", w2_grouped, [slice(0, H)])

        picked_words = sb("picked_words", [P, V + S], U32, tag="w2_grouped")
        two_words = picked_words[:, :V]
        offs_words = picked_words[:, V:]
        nc.vector.tensor_copy(two_words, x_table[:].indirect(two_list[:]))
        nc.vector.tensor_copy(offs_words.rearrange("p (t m) -> p m t", t=PACK), x_table[:].indirect(offs_list[:]))

        w1_grouped = sb("w1_grouped", [P, PACK * H], BF16)
        deal(nc.scalar.copy, w1_grouped, 0, w1_raw[0][:])
        deal(nc.vector.tensor_copy, w1_grouped, P // 2, w1_raw[1][:])
        w1_codes, w1_scales = quantize_weights("w1", w1_grouped, [slice(0, H // 2), slice(H // 2, H)])

        z2_planes = sb("z2_planes", [P, 2, PACK, HALF], BF16, tag="w1_raw0")
        for h in range(2):
            cols = slice(h * HALF, (h + 1) * HALF)
            for u in range(2):
                acc = bank(2 * h + u, [P, 2, HALF])
                for e in range(2):
                    j = 2 * u + e
                    feats = slice(j * P, (j + 1) * P)
                    product(acc[:, e, :], w2_codes[:, feats], w2_scales[:, feats], two_words[:, cols], two_scales[:, cols])
                for e in range(2):
                    j = 2 * u + e
                    nc.scalar.activation(out=z2_planes[:, h, j, :], in_=acc[:, e, :], func=ACT.Copy, scale=gb_t[:, j : j + 1])

        def project_a(t):
            cols = slice(t * P, (t + 1) * P)
            acc = bank(4 + min(t, 1), [P, PACK, P])
            for j in range(PACK):
                feats = slice(j * P, (j + 1) * P)
                product(acc[:, j, :], w1_codes[:, feats], w1_scales[:, feats], offs_words[:, cols], offs_scales[:, cols])
            return acc

        def interleave(copy, grouped, planes):
            copy(
                grouped[:].rearrange("p (c i j) -> p c j i", i=4, j=PACK),
                planes.rearrange("p j (c i) -> p c j i", i=4),
            )

        z2_codes = sb("z2_codes", [P, V], U32)
        z2_scales = sb("z2_scales", [P, V], U8)
        z2_grouped = [sb("z2_grouped%d" % h, [P, PACK * HALF], BF16) for h in range(2)]

        def quantize_z2(h):
            cols = slice(h * HALF, (h + 1) * HALF)
            nc.vector.quantize_mx(out=z2_codes[:, cols].bitcast(FP8X4), scales=z2_scales[:, cols], in_=z2_grouped[h][:])

        z_grouped = [sb("z_grouped%d" % t, [P, PACK * P], BF16) for t in range(PACK)]
        z_codes = [sb("z_codes%d" % t, [P, P], U32) for t in range(PACK)]
        z_scales = [sb("z_scales%d" % t, [P, P], U8) for t in range(PACK)]

        def weigh_on_scalar(t):
            acc = project_a(t)
            planes = sb("z_planes%d" % t, [P, PACK, P], BF16, tag="z_grouped0" if t == 1 else None)
            for j in range(PACK):
                nc.scalar.activation(out=planes[:, j, :], in_=acc[:, j, :], func=ACT.Copy, scale=ga_t[:, j : j + 1])
            interleave(nc.scalar.copy, z_grouped[t], planes[:])

        def quantize_z(t):
            nc.vector.quantize_mx(out=z_codes[t][:].bitcast(FP8X4), scales=z_scales[t][:], in_=z_grouped[t][:])

        interleave(nc.vector.tensor_copy, z2_grouped[0], z2_planes[:, 0])
        interleave(nc.scalar.copy, z2_grouped[1], z2_planes[:, 1])
        nc.vector.tensor_tensor(
            out=z_grouped[0][:].rearrange("p (m j) -> p m j", j=PACK),
            in0=project_a(0)[:].rearrange("p j m -> p m j"),
            in1=ga_t[:].unsqueeze(1).to_broadcast([P, P, PACK]),
            op=ALU.mult,
        )
        quantize_z2(0)
        quantize_z(0)
        quantize_z2(1)

        def put(t, cols, bank_index, tag):
            width = cols.stop - cols.start
            scores = bank(bank_index, [P, width])
            product(scores[:], z_codes[t][:], z_scales[t][:], z2_codes[:, cols], z2_scales[:, cols])
            tanh = sb("tanh%d_%d" % (t, cols.start), [P, width], F32, tag=tag)
            nc.scalar.activation(out=tanh[:], in_=scores[:], func=ACT.Tanh, scale=0.0625)
            nc.vector.tensor_copy(windows[t][:].indirect(slot_list[:, cols.start // 16 : cols.stop // 16]), tanh[:])

        for t in range(PACK):
            halved = t < 2
            if halved:
                put(t, slice(0, HALF), 6 - 6 * t, None)
            if t + 1 < PACK:
                weigh_on_scalar(t + 1)
                quantize_z(t + 1)
            tag = "z_grouped0" if t == 0 else "z_planes%d" % (t + 1)
            put(t, slice(HALF if halved else 0, V), [7, 1, 2, 3][t], tag)
            nc.sync.dma_start(out_rows[t], windows[t][:])
